import numpy as np
import ml_dtypes


def mxq(x, axis, fmt="e4m3"):
    dtype, down = {"e4m3": (ml_dtypes.float8_e4m3fn, 7), "e5m2": (ml_dtypes.float8_e5m2, 14)}[fmt]
    v = np.moveaxis(np.asarray(x, np.float32).astype(ml_dtypes.bfloat16).astype(np.float64), axis, -1)
    blocks = v.reshape(v.shape[:-1] + (-1, 32))
    amax = np.abs(blocks).max(-1, keepdims=True)
    byte = np.maximum(np.where(amax > 0, np.frexp(amax)[1] - 1 + 127, 0) - down, 1)
    scale = np.exp2(byte - 127.0)
    codes = (blocks / scale).astype(np.float32).astype(dtype).astype(np.float64)
    return np.moveaxis((codes * scale).reshape(v.shape), -1, axis)


WIDE = False


def mx_kscale(k):
    if not WIDE:
        return np.ones(k)
    levels = np.array([10, -10, 5, -5, 0])
    if k % 512:
        return np.exp2(np.random.permutation(np.resize(levels, k // 32))).repeat(32)
    a = np.empty((k // 512, 16))
    for p in range(k // 512):
        a[p, :8] = np.random.permutation(np.resize(levels, 8))
        for g in range(8):
            far = levels[np.abs(levels - a[p, g]) >= 10]
            a[p, g + 8] = far[np.random.randint(len(far))]
    return np.exp2(a.ravel()).repeat(32)


def f64(x):
    return np.asarray(x).astype(np.float64)


def striped(idx):
    return np.tile(idx.reshape(-1, 16).T, (8, 1)).astype(np.uint16)


def unstriped(offs):
    return offs[:16].T.reshape(-1).astype(np.int64)


E2M1 = np.array([0.0, 0.5, 1.0, 1.5, 2.0, 3.0, 4.0, 6.0, -0.0, -0.5, -1.0, -1.5, -2.0, -3.0, -4.0, -6.0])


def pack_fp4(w):
    k, n = w.shape
    w = f64(np.asarray(w, np.float32).astype(ml_dtypes.bfloat16)).reshape(k // 32, 32, n)
    amax = np.abs(w).max(1)
    mant, ex = np.frexp(amax / 6.0)
    byte = np.clip(np.where(amax > 0, np.where(mant > 0.5, ex, ex - 1) + 127, 1), 1, 254)
    scaled = (w * np.exp2(127.0 - byte)[:, None, :]).reshape(k, n).astype(np.float32)
    c = np.ascontiguousarray(scaled.reshape(k // 512, 128, 4, n).transpose(0, 1, 3, 2)).astype(ml_dtypes.float4_e2m1fn).view(np.uint8) & 0xF
    words = (c[..., 0::2] | (c[..., 1::2] << 4)).reshape(k // 512, 128, 2 * n)
    return np.ascontiguousarray(words), np.ascontiguousarray(byte.astype(np.uint8).reshape(k // 512, 16, n))


def unpack_fp4(words, scales):
    g, _, n = scales.shape
    words = np.ascontiguousarray(words).reshape(g, 128, n, 2)
    nib = np.empty((g, 128, n, 4), np.uint8)
    nib[..., 0::2] = words & 0xF
    nib[..., 1::2] = words >> 4
    vals = E2M1[nib] * np.repeat(np.exp2(scales.astype(np.float64) - 127.0), 8, axis=1)[..., None]
    return vals.transpose(0, 1, 3, 2).reshape(g * 512, n)


K, T, S, N = 512, 2048, 1024, 128
P = 2 ** 7


def setup_inputs():
    n = np.random.standard_normal
    s = mx_kscale(K)[:, None]
    packed_w1 = pack_fp4(n((K, N)) / np.sqrt(K) / s)
    return {
        "xT": (n((K, T)) * s).astype(np.float32),
        "w1_words": packed_w1[0],
        "w1_scales": packed_w1[1],
        "prior": np.tile(0.5 * np.random.standard_normal(S), (P, 1)).astype(np.float32),
        "offs": striped(np.random.permutation(T)[:S]),
    }


def reference(xT, w1_words, w1_scales, prior, offs):
    xq = mxq(f64(xT)[:, unstriped(offs)], 0, "e4m3")
    y = unpack_fp4(w1_words, w1_scales).T @ xq
    yp = y + f64(prior)[:1]
    e = np.exp(yp - yp.max(axis=1, keepdims=True))
    return e / e.sum(axis=1, keepdims=True)

@@ -1,0 +1,142 @@
+from contextlib import ExitStack
+
+import concourse.mybir as mybir
+
+K, T, S, N = 512, 2048, 1024, 128
+FLOPS = 2 * K * S * N
+
+F32 = mybir.dt.float32
+BF16 = mybir.dt.bfloat16
+I32 = mybir.dt.int32
+U32 = mybir.dt.uint32
+U16 = mybir.dt.uint16
+U8 = mybir.dt.uint8
+FP8X4 = mybir.dt.float8_e4m3fn_x4
+FP4X4 = mybir.dt.float4_e2m1fn_x4
+ALU = mybir.AluOpType
+ACT = mybir.ActivationFunctionType
+AX = mybir.AxisListType
+
+P = 128
+CH = 256
+NCH = S // CH
+FIRST_CUTS = (0, 1024, 2048)
+PAIR_CUTS = (0, 1024, 1536, 1792, 2048)
+LAST_CUTS = (0, 512, 1024, 1536, 2048)
+
+
+def tile_picked_rank_prior_e_kernel(tc, xT, w1_words, w1_scales, prior, offs, out):
+    nc = tc.nc
+    rows = xT.rearrange("(p j) t -> p j t", j=4)
+    with ExitStack() as ctx:
+        keep = ctx.enter_context(tc.tile_pool(name="keep", bufs=1))
+        ring = ctx.enter_context(tc.tile_pool(name="ring", bufs=2))
+        psum = ctx.enter_context(tc.psum_pool(name="psum", bufs=1))
+
+        offsets = keep.tile([P, S // 16], U16, name="offsets")
+
+        warm_in = keep.tile([P, 1], F32, name="warm_in")
+        warm_out = keep.tile([P, 1], F32, name="warm_out")
+        nc.vector.memset(warm_in[:], 0.0)
+        nc.scalar.activation(warm_out[:], warm_in[:], ACT.Exp)
+
+        w_scale = keep.tile([P, N], U8, name="w_scale", align_bytes=64)
+        nc.vector.memset(w_scale[:].bitcast(I32), 0)
+
+        grouped = [keep.tile([P, CH, 4], BF16, name="grouped%d" % c, align_bytes=64) for c in range(NCH)]
+
+        def chunk_offsets(c):
+            return offsets[:, c * CH // 16 : (c + 1) * CH // 16]
+
+        def single_plane(j, cuts):
+            plane = keep.tile([P, T], BF16, name="plane%d" % j)
+            for a, b in zip(cuts[:-1], cuts[1:]):
+                raw = keep.tile([P, b - a], F32, name="raw%d_%d" % (j, a))
+                nc.sync.dma_start(raw[:], rows[:, j, a:b])
+                nc.scalar.activation(plane[:, a:b], raw[:], ACT.Copy)
+            return plane
+
+        def gather_plane(j, plane, c):
+            nc.scalar.activation(grouped[c][:, :, j], plane[:].indirect(chunk_offsets(c)), ACT.Copy)
+
+        plane2 = single_plane(2, FIRST_CUTS)
+        nc.sync.dma_start(offsets[:], offs)
+        for c in range(NCH):
+            gather_plane(2, plane2, c)
+
+        pairs = keep.tile([P, T, 2], BF16, name="pairs")
+        for a, b in zip(PAIR_CUTS[:-1], PAIR_CUTS[1:]):
+            raw = keep.tile([P, 2, b - a], F32, name="rawp_%d" % a)
+            nc.sync.dma_start(raw[:], rows[:, 0:2, a:b])
+            nc.vector.tensor_copy(pairs[:, a:b, :], raw[:].rearrange("p e t -> p t e"))
+        pair_words = pairs[:].rearrange("p t e -> p (t e)").bitcast(U32)
+        for c in range(NCH):
+            words = grouped[c][:].rearrange("p n t -> p (n t)").bitcast(U32).rearrange("p (n u) -> p n u", u=2)
+            nc.vector.tensor_copy(words[:, :, 0], pair_words.indirect(chunk_offsets(c)))
+
+        plane3 = single_plane(3, LAST_CUTS)
+        w_codes = keep.tile([P, 2 * N], U8, name="w_codes", align_bytes=64)
+        nc.sync.dma_start(w_codes[:].bitcast(I32), w1_words[0].bitcast(I32))
+        for q in range(4):
+            nc.sync.dma_start(w_scale[32 * q : 32 * q + 4, :].bitcast(I32), w1_scales[0, 4 * q : 4 * q + 4, :].bitcast(I32))
+
+        prior_sb = keep.tile([P, S], F32, name="prior_sb")
+        nc.sync.dma_start(prior_sb[:], prior)
+
+        neg_max = keep.tile([P, NCH], F32, name="neg_max")
+        sums = keep.tile([P, NCH], F32, name="sums")
+        neg = [keep.tile([P, CH], F32, name="neg%d" % c) for c in range(NCH)]
+        ex = [keep.tile([P, CH], F32, name="ex%d" % c) for c in range(NCH)]
+        acc = [psum.tile([P, CH], F32, name="acc%d" % c) for c in range(NCH)]
+        passed = keep.tile([P, CH], BF16, name="passed")
+        factor = keep.tile([P, NCH - 1], F32, name="factor")
+        for c in range(NCH):
+            gather_plane(3, plane3, c)
+
+        def product(c):
+            codes = ring.tile([P, CH], U32, name="codes", align_bytes=64)
+            scales = ring.tile([P, CH], U8, name="scales", align_bytes=64)
+            nc.vector.quantize_mx(out=codes[:].bitcast(FP8X4), scales=scales[:], in_=grouped[c][:].rearrange("p n t -> p (n t)"))
+            nc.tensor.matmul_mx(out=acc[c][:], lhsT=w_codes[:].bitcast(FP4X4), lhsT_scale=w_scale[:],
+                                rhs=codes[:].bitcast(FP8X4), rhs_scale=scales[:], start=True, stop=True)
+
+        def add_prior(c):
+            nc.vector.scalar_tensor_tensor(neg[c][:], acc[c][:], -1.0, prior_sb[:, c * CH : (c + 1) * CH], ALU.mult, ALU.subtract)
+
+        def running_max(c):
+            if c == 0:
+                nc.vector.tensor_reduce(neg_max[:, 0:1], neg[0][:], AX.X, ALU.min)
+            else:
+                nc.vector.tensor_scalar(passed[:], neg[c][:], 1.0, neg_max[:, c - 1 : c], ALU.mult, ALU.min, accum_out=neg_max[:, c : c + 1])
+            if c == NCH - 1:
+                nc.scalar.activation(factor[:], neg_max[:, : NCH - 1], ACT.Exp, bias=neg_max[:, c : c + 1], scale=-1.0)
+            nc.scalar.activation(ex[c][:], neg[c][:], ACT.Exp, bias=neg_max[:, c : c + 1], scale=-1.0, accum_out=sums[:, c : c + 1])
+
+        product(0)
+        product(1)
+        add_prior(0)
+        product(2)
+        running_max(0)
+        add_prior(1)
+        product(3)
+        running_max(1)
+        add_prior(2)
+        add_prior(3)
+        running_max(2)
+        running_max(3)
+
+        weighted = keep.tile([P, NCH - 1], F32, name="weighted")
+        early = keep.tile([P, 1], F32, name="early")
+        nc.vector.scalar_tensor_tensor(weighted[:], sums[:, : NCH - 1], 1.0, factor[:], ALU.mult, ALU.mult, accum_out=early[:])
+        total = keep.tile([P, 1], F32, name="total")
+        nc.vector.tensor_tensor(total[:], early[:], sums[:, NCH - 1 : NCH], ALU.add)
+        inv = keep.tile([P, 1], F32, name="inv")
+        nc.vector.reciprocal(inv[:], total[:])
+        for c in range(NCH):
+            res = keep.tile([P, CH], F32, name="res%d" % c)
+            if c < NCH - 1:
+                nc.vector.tensor_scalar(res[:], ex[c][:], factor[:, c : c + 1], inv[:], ALU.mult, ALU.mult)
+                nc.sync.dma_start(out[:, c * CH : (c + 1) * CH], res[:])
+            else:
+                nc.scalar.activation(res[:], ex[c][:], ACT.Copy, scale=inv[:])
+                nc.scalar.dma_start(out[:, c * CH : (c + 1) * CH], res[:])

@@ -23,6 +23,8 @@ NCH = S // CH
 FIRST_CUTS = (0, 1024, 2048)
 PAIR_CUTS = (0, 1024, 1536, 1792, 2048)
 LAST_CUTS = (0, 512, 1024, 1536, 2048)
+V2 = 2
+SCALAR_PAIR = (1024,)
 
 
 def tile_picked_rank_prior_e_kernel(tc, xT, w1_words, w1_scales, prior, offs, out):
@@ -48,50 +50,56 @@ def tile_picked_rank_prior_e_kernel(tc, xT, w1_words, w1_scales, prior, offs, ou
         def chunk_offsets(c):
             return offsets[:, c * CH // 16 : (c + 1) * CH // 16]
 
-        def single_plane(j, cuts):
-            plane = keep.tile([P, T], BF16, name="plane%d" % j)
-            for a, b in zip(cuts[:-1], cuts[1:]):
-                raw = keep.tile([P, b - a], F32, name="raw%d_%d" % (j, a))
-                nc.sync.dma_start(raw[:], rows[:, j, a:b])
-                nc.scalar.activation(plane[:, a:b], raw[:], ACT.Copy)
-            return plane
-
-        def gather_plane(j, plane, c):
-            nc.scalar.activation(grouped[c][:, :, j], plane[:].indirect(chunk_offsets(c)), ACT.Copy)
-
-        plane2 = single_plane(2, FIRST_CUTS)
+        raw2 = keep.tile([P, T], F32, name="raw2", tag="reused")
+        plane2 = keep.tile([P, T], BF16, name="plane2")
+        for a, b in zip(FIRST_CUTS[:-1], FIRST_CUTS[1:]):
+            nc.sync.dma_start(raw2[:, a:b], rows[:, 2, a:b])
+            nc.vector.tensor_copy(plane2[:, a:b], raw2[:, a:b])
         nc.sync.dma_start(offsets[:], offs)
         for c in range(NCH):
-            gather_plane(2, plane2, c)
+            if c < V2:
+                nc.vector.tensor_copy(grouped[c][:, :, 2], raw2[:].indirect(chunk_offsets(c)))
+            else:
+                nc.scalar.activation(grouped[c][:, :, 2], plane2[:].indirect(chunk_offsets(c)), ACT.Copy)
 
         pairs = keep.tile([P, T, 2], BF16, name="pairs")
         for a, b in zip(PAIR_CUTS[:-1], PAIR_CUTS[1:]):
             raw = keep.tile([P, 2, b - a], F32, name="rawp_%d" % a)
             nc.sync.dma_start(raw[:], rows[:, 0:2, a:b])
-            nc.vector.tensor_copy(pairs[:, a:b, :], raw[:].rearrange("p e t -> p t e"))
+            dst = pairs[:, a:b, :].rearrange("p (c i) e -> p c e i", i=4)
+            src = raw[:].rearrange("p e (c i) -> p c e i", i=4)
+            if a in SCALAR_PAIR:
+                nc.scalar.activation(dst, src, ACT.Copy)
+            else:
+                nc.vector.tensor_copy(dst, src)
         pair_words = pairs[:].rearrange("p t e -> p (t e)").bitcast(U32)
         for c in range(NCH):
             words = grouped[c][:].rearrange("p n t -> p (n t)").bitcast(U32).rearrange("p (n u) -> p n u", u=2)
             nc.vector.tensor_copy(words[:, :, 0], pair_words.indirect(chunk_offsets(c)))
 
-        plane3 = single_plane(3, LAST_CUTS)
+        plane3 = keep.tile([P, T], BF16, name="plane3", tag="reused")
+        for a, b in zip(LAST_CUTS[:-1], LAST_CUTS[1:]):
+            raw = keep.tile([P, b - a], F32, name="raw3_%d" % a)
+            nc.sync.dma_start(raw[:], rows[:, 3, a:b])
+            nc.scalar.activation(plane3[:, a:b], raw[:], ACT.Copy)
+
+        prior_row = keep.tile([P, S], F32, name="prior_row")
+        nc.sync.dma_start(prior_row[:], prior)
         w_codes = keep.tile([P, 2 * N], U8, name="w_codes", align_bytes=64)
         nc.sync.dma_start(w_codes[:].bitcast(I32), w1_words[0].bitcast(I32))
         for q in range(4):
             nc.sync.dma_start(w_scale[32 * q : 32 * q + 4, :].bitcast(I32), w1_scales[0, 4 * q : 4 * q + 4, :].bitcast(I32))
 
-        prior_sb = keep.tile([P, S], F32, name="prior_sb")
-        nc.sync.dma_start(prior_sb[:], prior)
-
+        last = NCH - 1
         neg_max = keep.tile([P, NCH], F32, name="neg_max")
         sums = keep.tile([P, NCH], F32, name="sums")
         neg = [keep.tile([P, CH], F32, name="neg%d" % c) for c in range(NCH)]
         ex = [keep.tile([P, CH], F32, name="ex%d" % c) for c in range(NCH)]
         acc = [psum.tile([P, CH], F32, name="acc%d" % c) for c in range(NCH)]
         passed = keep.tile([P, CH], BF16, name="passed")
-        factor = keep.tile([P, NCH - 1], F32, name="factor")
+        factor = keep.tile([P, last], F32, name="factor")
         for c in range(NCH):
-            gather_plane(3, plane3, c)
+            nc.scalar.activation(grouped[c][:, :, 3], plane3[:].indirect(chunk_offsets(c)), ACT.Copy)
 
         def product(c):
             codes = ring.tile([P, CH], U32, name="codes", align_bytes=64)
@@ -101,15 +109,15 @@ def tile_picked_rank_prior_e_kernel(tc, xT, w1_words, w1_scales, prior, offs, ou
                                 rhs=codes[:].bitcast(FP8X4), rhs_scale=scales[:], start=True, stop=True)
 
         def add_prior(c):
-            nc.vector.scalar_tensor_tensor(neg[c][:], acc[c][:], -1.0, prior_sb[:, c * CH : (c + 1) * CH], ALU.mult, ALU.subtract)
+            nc.vector.scalar_tensor_tensor(neg[c][:], acc[c][:], -1.0, prior_row[:, c * CH : (c + 1) * CH], ALU.mult, ALU.subtract)
 
         def running_max(c):
             if c == 0:
                 nc.vector.tensor_reduce(neg_max[:, 0:1], neg[0][:], AX.X, ALU.min)
             else:
                 nc.vector.tensor_scalar(passed[:], neg[c][:], 1.0, neg_max[:, c - 1 : c], ALU.mult, ALU.min, accum_out=neg_max[:, c : c + 1])
-            if c == NCH - 1:
-                nc.scalar.activation(factor[:], neg_max[:, : NCH - 1], ACT.Exp, bias=neg_max[:, c : c + 1], scale=-1.0)
+            if c == last:
+                nc.scalar.activation(factor[:], neg_max[:, :last], ACT.Exp, bias=neg_max[:, c : c + 1], scale=-1.0)
             nc.scalar.activation(ex[c][:], neg[c][:], ACT.Exp, bias=neg_max[:, c : c + 1], scale=-1.0, accum_out=sums[:, c : c + 1])
 
         product(0)
@@ -125,16 +133,16 @@ def tile_picked_rank_prior_e_kernel(tc, xT, w1_words, w1_scales, prior, offs, ou
         running_max(2)
         running_max(3)
 
-        weighted = keep.tile([P, NCH - 1], F32, name="weighted")
+        weighted = keep.tile([P, last], F32, name="weighted")
         early = keep.tile([P, 1], F32, name="early")
-        nc.vector.scalar_tensor_tensor(weighted[:], sums[:, : NCH - 1], 1.0, factor[:], ALU.mult, ALU.mult, accum_out=early[:])
+        nc.vector.scalar_tensor_tensor(weighted[:], sums[:, :last], 1.0, factor[:], ALU.mult, ALU.mult, accum_out=early[:])
         total = keep.tile([P, 1], F32, name="total")
-        nc.vector.tensor_tensor(total[:], early[:], sums[:, NCH - 1 : NCH], ALU.add)
+        nc.vector.tensor_tensor(total[:], early[:], sums[:, last : last + 1], ALU.add)
         inv = keep.tile([P, 1], F32, name="inv")
         nc.vector.reciprocal(inv[:], total[:])
         for c in range(NCH):
             res = keep.tile([P, CH], F32, name="res%d" % c)
-            if c < NCH - 1:
+            if c < last:
                 nc.vector.tensor_scalar(res[:], ex[c][:], factor[:, c : c + 1], inv[:], ALU.mult, ALU.mult)
                 nc.sync.dma_start(out[:, c * CH : (c + 1) * CH], res[:])
             else:

@@ -21,10 +21,10 @@ P = 128
 CH = 256
 NCH = S // CH
 FIRST_CUTS = (0, 1024, 2048)
-PAIR_CUTS = (0, 1024, 1536, 1792, 2048)
+PAIR_CUTS = (0, 1024, 1536, 2048)
 LAST_CUTS = (0, 512, 1024, 1536, 2048)
 V2 = 2
-SCALAR_PAIR = (1024,)
+SCALAR_COLS = 160
 
 
 def tile_picked_rank_prior_e_kernel(tc, xT, w1_words, w1_scales, prior, offs, out):
@@ -66,12 +66,17 @@ def tile_picked_rank_prior_e_kernel(tc, xT, w1_words, w1_scales, prior, offs, ou
         for a, b in zip(PAIR_CUTS[:-1], PAIR_CUTS[1:]):
             raw = keep.tile([P, 2, b - a], F32, name="rawp_%d" % a)
             nc.sync.dma_start(raw[:], rows[:, 0:2, a:b])
-            dst = pairs[:, a:b, :].rearrange("p (c i) e -> p c e i", i=4)
-            src = raw[:].rearrange("p e (c i) -> p c e i", i=4)
-            if a in SCALAR_PAIR:
-                nc.scalar.activation(dst, src, ACT.Copy)
-            else:
-                nc.vector.tensor_copy(dst, src)
+            mid = b - SCALAR_COLS if b == T else b
+            nc.vector.tensor_copy(
+                pairs[:, a:mid, :].rearrange("p (c i) e -> p c e i", i=4),
+                raw[:, :, : mid - a].rearrange("p e (c i) -> p c e i", i=4),
+            )
+            if mid < b:
+                nc.scalar.activation(
+                    pairs[:, mid:b, :].rearrange("p (c i) e -> p c e i", i=4),
+                    raw[:, :, mid - a :].rearrange("p e (c i) -> p c e i", i=4),
+                    ACT.Copy,
+                )
         pair_words = pairs[:].rearrange("p t e -> p (t e)").bitcast(U32)
         for c in range(NCH):
             words = grouped[c][:].rearrange("p n t -> p (n t)").bitcast(U32).rearrange("p (n u) -> p n u", u=2)
@@ -90,16 +95,19 @@ def tile_picked_rank_prior_e_kernel(tc, xT, w1_words, w1_scales, prior, offs, ou
         for q in range(4):
             nc.sync.dma_start(w_scale[32 * q : 32 * q + 4, :].bitcast(I32), w1_scales[0, 4 * q : 4 * q + 4, :].bitcast(I32))
 
-        last = NCH - 1
-        neg_max = keep.tile([P, NCH], F32, name="neg_max")
-        sums = keep.tile([P, NCH], F32, name="sums")
-        neg = [keep.tile([P, CH], F32, name="neg%d" % c) for c in range(NCH)]
-        ex = [keep.tile([P, CH], F32, name="ex%d" % c) for c in range(NCH)]
+        first_max = keep.tile([P, 1], F32, name="first_max")
+        sums = keep.tile([P, 3], F32, name="sums")
+        neg = keep.tile([P, S + 3], F32, name="neg")
+        ex = keep.tile([P, S + 3], F32, name="ex")
         acc = [psum.tile([P, CH], F32, name="acc%d" % c) for c in range(NCH)]
         passed = keep.tile([P, CH], BF16, name="passed")
-        factor = keep.tile([P, last], F32, name="factor")
+        neg_max = [first_max[:]] + [neg[:, S + s : S + s + 1] for s in range(3)]
+        factor = ex[:, S:]
         for c in range(NCH):
             nc.scalar.activation(grouped[c][:, :, 3], plane3[:].indirect(chunk_offsets(c)), ACT.Copy)
+
+        def cols(c):
+            return slice(c * CH, (c + 1) * CH)
 
         def product(c):
             codes = ring.tile([P, CH], U32, name="codes", align_bytes=64)
@@ -109,16 +117,19 @@ def tile_picked_rank_prior_e_kernel(tc, xT, w1_words, w1_scales, prior, offs, ou
                                 rhs=codes[:].bitcast(FP8X4), rhs_scale=scales[:], start=True, stop=True)
 
         def add_prior(c):
-            nc.vector.scalar_tensor_tensor(neg[c][:], acc[c][:], -1.0, prior_row[:, c * CH : (c + 1) * CH], ALU.mult, ALU.subtract)
+            nc.vector.scalar_tensor_tensor(neg[:, cols(c)], acc[c][:], -1.0, prior_row[:, cols(c)], ALU.mult, ALU.subtract)
 
         def running_max(c):
             if c == 0:
-                nc.vector.tensor_reduce(neg_max[:, 0:1], neg[0][:], AX.X, ALU.min)
+                nc.vector.tensor_reduce(neg_max[0], neg[:, cols(0)], AX.X, ALU.min)
             else:
-                nc.vector.tensor_scalar(passed[:], neg[c][:], 1.0, neg_max[:, c - 1 : c], ALU.mult, ALU.min, accum_out=neg_max[:, c : c + 1])
-            if c == last:
-                nc.scalar.activation(factor[:], neg_max[:, :last], ACT.Exp, bias=neg_max[:, c : c + 1], scale=-1.0)
-            nc.scalar.activation(ex[c][:], neg[c][:], ACT.Exp, bias=neg_max[:, c : c + 1], scale=-1.0, accum_out=sums[:, c : c + 1])
+                nc.vector.tensor_scalar(passed[:], neg[:, cols(c)], 1.0, neg_max[c - 1], ALU.mult, ALU.min, accum_out=neg_max[c])
+
+        spans = (slice(0, 2 * CH), cols(2), cols(3))
+
+        def exponentials(s):
+            wide = slice(spans[s].start, S + 3) if s == 2 else spans[s]
+            nc.scalar.activation(ex[:, wide], neg[:, wide], ACT.Exp, bias=neg_max[s + 1], scale=-1.0, accum_out=sums[:, s : s + 1])
 
         product(0)
         product(1)
@@ -128,23 +139,22 @@ def tile_picked_rank_prior_e_kernel(tc, xT, w1_words, w1_scales, prior, offs, ou
         add_prior(1)
         product(3)
         running_max(1)
+        exponentials(0)
         add_prior(2)
         add_prior(3)
         running_max(2)
+        exponentials(1)
         running_max(3)
+        exponentials(2)
 
-        weighted = keep.tile([P, last], F32, name="weighted")
-        early = keep.tile([P, 1], F32, name="early")
-        nc.vector.scalar_tensor_tensor(weighted[:], sums[:, :last], 1.0, factor[:], ALU.mult, ALU.mult, accum_out=early[:])
+        weighted = keep.tile([P, 3], F32, name="weighted")
         total = keep.tile([P, 1], F32, name="total")
-        nc.vector.tensor_tensor(total[:], early[:], sums[:, last : last + 1], ALU.add)
+        nc.vector.scalar_tensor_tensor(weighted[:], sums[:], 1.0, factor, ALU.subtract, ALU.mult, accum_out=total[:])
         inv = keep.tile([P, 1], F32, name="inv")
         nc.vector.reciprocal(inv[:], total[:])
-        for c in range(NCH):
-            res = keep.tile([P, CH], F32, name="res%d" % c)
-            if c < last:
-                nc.vector.tensor_scalar(res[:], ex[c][:], factor[:, c : c + 1], inv[:], ALU.mult, ALU.mult)
-                nc.sync.dma_start(out[:, c * CH : (c + 1) * CH], res[:])
-            else:
-                nc.scalar.activation(res[:], ex[c][:], ACT.Copy, scale=inv[:])
-                nc.scalar.dma_start(out[:, c * CH : (c + 1) * CH], res[:])
+        res = keep.tile([P, S], F32, name="res")
+        for s in (1, 0):
+            nc.vector.tensor_scalar(res[:, spans[s]], ex[:, spans[s]], factor[:, s : s + 1], inv[:], ALU.mult, ALU.mult)
+            nc.sync.dma_start(out[:, spans[s]], res[:, spans[s]])
+        nc.scalar.activation(res[:, spans[2]], ex[:, spans[2]], ACT.Copy, scale=inv[:])
+        nc.scalar.dma_start(out[:, spans[2]], res[:, spans[2]])

@@ -18,18 +18,26 @@ ACT = mybir.ActivationFunctionType
 AX = mybir.AxisListType
 
 P = 128
-CH = 256
-NCH = S // CH
-FIRST_CUTS = (0, 1024, 2048)
+PACK = 4
+CHUNK = 256
+CHUNKS = S // CHUNK
+
+PLANE2_CUTS = (0, 1024, 2048)
 PAIR_CUTS = (0, 1024, 1536, 2048)
-LAST_CUTS = (0, 512, 1024, 1536, 2048)
-V2 = 2
-SCALAR_COLS = 160
+PLANE3_CUTS = (0, 512, 1024, 1536, 2048)
+PLANE2_VECTOR_CHUNKS = 2
+PAIR_SCALAR_COLS = (0, 256, 160)
+SPANS = (slice(0, 2 * CHUNK), slice(2 * CHUNK, 3 * CHUNK), slice(3 * CHUNK, 4 * CHUNK))
+LAST = len(SPANS) - 1
+
+
+def pieces(cuts):
+    return zip(cuts[:-1], cuts[1:])
 
 
 def tile_picked_rank_prior_e_kernel(tc, xT, w1_words, w1_scales, prior, offs, out):
     nc = tc.nc
-    rows = xT.rearrange("(p j) t -> p j t", j=4)
+    planes = xT.rearrange("(p t) c -> p t c", t=PACK)
     with ExitStack() as ctx:
         keep = ctx.enter_context(tc.tile_pool(name="keep", bufs=1))
         ring = ctx.enter_context(tc.tile_pool(name="ring", bufs=2))
@@ -37,99 +45,105 @@ def tile_picked_rank_prior_e_kernel(tc, xT, w1_words, w1_scales, prior, offs, ou
 
         offsets = keep.tile([P, S // 16], U16, name="offsets")
 
-        warm_in = keep.tile([P, 1], F32, name="warm_in")
-        warm_out = keep.tile([P, 1], F32, name="warm_out")
-        nc.vector.memset(warm_in[:], 0.0)
-        nc.scalar.activation(warm_out[:], warm_in[:], ACT.Exp)
+        def chunk_offsets(c):
+            return offsets[:, c * CHUNK // 16 : (c + 1) * CHUNK // 16]
+
+        def chunk_cols(c):
+            return slice(c * CHUNK, (c + 1) * CHUNK)
 
         w_scale = keep.tile([P, N], U8, name="w_scale", align_bytes=64)
         nc.vector.memset(w_scale[:].bitcast(I32), 0)
 
-        grouped = [keep.tile([P, CH, 4], BF16, name="grouped%d" % c, align_bytes=64) for c in range(NCH)]
+        grouped = [keep.tile([P, CHUNK, PACK], BF16, name="grouped%d" % c, align_bytes=64) for c in range(CHUNKS)]
 
-        def chunk_offsets(c):
-            return offsets[:, c * CH // 16 : (c + 1) * CH // 16]
-
-        raw2 = keep.tile([P, T], F32, name="raw2", tag="reused")
+        raw2 = keep.tile([P, T], F32, name="raw2", tag="raw2_then_plane3")
         plane2 = keep.tile([P, T], BF16, name="plane2")
-        for a, b in zip(FIRST_CUTS[:-1], FIRST_CUTS[1:]):
-            nc.sync.dma_start(raw2[:, a:b], rows[:, 2, a:b])
-            nc.vector.tensor_copy(plane2[:, a:b], raw2[:, a:b])
+        for a, b in pieces(PLANE2_CUTS):
+            nc.sync.dma_start(raw2[:, a:b], planes[:, 2, a:b])
+            nc.scalar.activation(plane2[:, a:b], raw2[:, a:b], ACT.Copy)
         nc.sync.dma_start(offsets[:], offs)
-        for c in range(NCH):
-            if c < V2:
+        for c in range(CHUNKS):
+            if c < PLANE2_VECTOR_CHUNKS:
                 nc.vector.tensor_copy(grouped[c][:, :, 2], raw2[:].indirect(chunk_offsets(c)))
             else:
                 nc.scalar.activation(grouped[c][:, :, 2], plane2[:].indirect(chunk_offsets(c)), ACT.Copy)
 
         pairs = keep.tile([P, T, 2], BF16, name="pairs")
-        for a, b in zip(PAIR_CUTS[:-1], PAIR_CUTS[1:]):
-            raw = keep.tile([P, 2, b - a], F32, name="rawp_%d" % a)
-            nc.sync.dma_start(raw[:], rows[:, 0:2, a:b])
-            mid = b - SCALAR_COLS if b == T else b
+        for (a, b), share in zip(pieces(PAIR_CUTS), PAIR_SCALAR_COLS):
+            raw01 = keep.tile([P, 2, b - a], F32, name="raw01_%d" % a)
+            nc.sync.dma_start(raw01[:], planes[:, 0:2, a:b])
+            mid = b - share
             nc.vector.tensor_copy(
                 pairs[:, a:mid, :].rearrange("p (c i) e -> p c e i", i=4),
-                raw[:, :, : mid - a].rearrange("p e (c i) -> p c e i", i=4),
+                raw01[:, :, : mid - a].rearrange("p e (c i) -> p c e i", i=4),
             )
             if mid < b:
                 nc.scalar.activation(
                     pairs[:, mid:b, :].rearrange("p (c i) e -> p c e i", i=4),
-                    raw[:, :, mid - a :].rearrange("p e (c i) -> p c e i", i=4),
+                    raw01[:, :, mid - a :].rearrange("p e (c i) -> p c e i", i=4),
                     ACT.Copy,
                 )
-        pair_words = pairs[:].rearrange("p t e -> p (t e)").bitcast(U32)
-        for c in range(NCH):
-            words = grouped[c][:].rearrange("p n t -> p (n t)").bitcast(U32).rearrange("p (n u) -> p n u", u=2)
+        pair_words = pairs[:].rearrange("p c e -> p (c e)").bitcast(U32)
+        for c in range(CHUNKS):
+            words = grouped[c][:].rearrange("p j t -> p (j t)").bitcast(U32).rearrange("p (j u) -> p j u", u=2)
             nc.vector.tensor_copy(words[:, :, 0], pair_words.indirect(chunk_offsets(c)))
 
-        plane3 = keep.tile([P, T], BF16, name="plane3", tag="reused")
-        for a, b in zip(LAST_CUTS[:-1], LAST_CUTS[1:]):
-            raw = keep.tile([P, b - a], F32, name="raw3_%d" % a)
-            nc.sync.dma_start(raw[:], rows[:, 3, a:b])
-            nc.scalar.activation(plane3[:, a:b], raw[:], ACT.Copy)
+        plane3 = keep.tile([P, T], BF16, name="plane3", tag="raw2_then_plane3")
+        for a, b in pieces(PLANE3_CUTS):
+            raw3 = keep.tile([P, b - a], F32, name="raw3_%d" % a)
+            nc.sync.dma_start(raw3[:], planes[:, 3, a:b])
+            nc.scalar.activation(plane3[:, a:b], raw3[:], ACT.Copy)
 
-        prior_row = keep.tile([P, S], F32, name="prior_row")
-        nc.sync.dma_start(prior_row[:], prior)
+        prior_sb = keep.tile([P, S], F32, name="prior_sb")
+        nc.sync.dma_start(prior_sb[:], prior)
         w_codes = keep.tile([P, 2 * N], U8, name="w_codes", align_bytes=64)
         nc.sync.dma_start(w_codes[:].bitcast(I32), w1_words[0].bitcast(I32))
         for q in range(4):
             nc.sync.dma_start(w_scale[32 * q : 32 * q + 4, :].bitcast(I32), w1_scales[0, 4 * q : 4 * q + 4, :].bitcast(I32))
 
         first_max = keep.tile([P, 1], F32, name="first_max")
-        sums = keep.tile([P, 3], F32, name="sums")
-        neg = keep.tile([P, S + 3], F32, name="neg")
-        ex = keep.tile([P, S + 3], F32, name="ex")
-        acc = [psum.tile([P, CH], F32, name="acc%d" % c) for c in range(NCH)]
-        passed = keep.tile([P, CH], BF16, name="passed")
-        neg_max = [first_max[:]] + [neg[:, S + s : S + s + 1] for s in range(3)]
+        sums = keep.tile([P, len(SPANS)], F32, name="sums")
+        neg = keep.tile([P, S + len(SPANS)], F32, name="neg")
+        ex = keep.tile([P, S + len(SPANS)], F32, name="ex")
+        acc = [psum.tile([P, CHUNK], F32, name="acc%d" % c) for c in range(CHUNKS)]
+        passed = keep.tile([P, CHUNK], BF16, name="passed")
+        neg_max = [first_max[:]] + [neg[:, S + s : S + s + 1] for s in range(len(SPANS))]
         factor = ex[:, S:]
-        for c in range(NCH):
+        for c in range(CHUNKS):
             nc.scalar.activation(grouped[c][:, :, 3], plane3[:].indirect(chunk_offsets(c)), ACT.Copy)
 
-        def cols(c):
-            return slice(c * CH, (c + 1) * CH)
-
         def product(c):
-            codes = ring.tile([P, CH], U32, name="codes", align_bytes=64)
-            scales = ring.tile([P, CH], U8, name="scales", align_bytes=64)
-            nc.vector.quantize_mx(out=codes[:].bitcast(FP8X4), scales=scales[:], in_=grouped[c][:].rearrange("p n t -> p (n t)"))
-            nc.tensor.matmul_mx(out=acc[c][:], lhsT=w_codes[:].bitcast(FP4X4), lhsT_scale=w_scale[:],
-                                rhs=codes[:].bitcast(FP8X4), rhs_scale=scales[:], start=True, stop=True)
+            codes = ring.tile([P, CHUNK], U32, name="codes", align_bytes=64)
+            scales = ring.tile([P, CHUNK], U8, name="scales", align_bytes=64)
+            nc.vector.quantize_mx(
+                out=codes[:].bitcast(FP8X4), scales=scales[:], in_=grouped[c][:].rearrange("p j t -> p (j t)")
+            )
+            nc.tensor.matmul_mx(
+                out=acc[c][:],
+                lhsT=w_codes[:].bitcast(FP4X4),
+                lhsT_scale=w_scale[:],
+                rhs=codes[:].bitcast(FP8X4),
+                rhs_scale=scales[:],
+                start=True,
+                stop=True,
+            )
 
         def add_prior(c):
-            nc.vector.scalar_tensor_tensor(neg[:, cols(c)], acc[c][:], -1.0, prior_row[:, cols(c)], ALU.mult, ALU.subtract)
+            cols = chunk_cols(c)
+            nc.vector.scalar_tensor_tensor(neg[:, cols], acc[c][:], -1.0, prior_sb[:, cols], ALU.mult, ALU.subtract)
 
         def running_max(c):
+            cols = chunk_cols(c)
             if c == 0:
-                nc.vector.tensor_reduce(neg_max[0], neg[:, cols(0)], AX.X, ALU.min)
+                nc.vector.tensor_reduce(neg_max[0], neg[:, cols], AX.X, ALU.min)
             else:
-                nc.vector.tensor_scalar(passed[:], neg[:, cols(c)], 1.0, neg_max[c - 1], ALU.mult, ALU.min, accum_out=neg_max[c])
-
-        spans = (slice(0, 2 * CH), cols(2), cols(3))
+                nc.vector.tensor_scalar(passed[:], neg[:, cols], 1.0, neg_max[c - 1], ALU.mult, ALU.min, accum_out=neg_max[c])
 
         def exponentials(s):
-            wide = slice(spans[s].start, S + 3) if s == 2 else spans[s]
-            nc.scalar.activation(ex[:, wide], neg[:, wide], ACT.Exp, bias=neg_max[s + 1], scale=-1.0, accum_out=sums[:, s : s + 1])
+            cols = slice(SPANS[s].start, S + len(SPANS)) if s == LAST else SPANS[s]
+            nc.scalar.activation(
+                ex[:, cols], neg[:, cols], ACT.Exp, bias=neg_max[s + 1], scale=-1.0, accum_out=sums[:, s : s + 1]
+            )
 
         product(0)
         product(1)
@@ -147,14 +161,15 @@ def tile_picked_rank_prior_e_kernel(tc, xT, w1_words, w1_scales, prior, offs, ou
         running_max(3)
         exponentials(2)
 
-        weighted = keep.tile([P, 3], F32, name="weighted")
+        weighted = keep.tile([P, len(SPANS)], F32, name="weighted")
         total = keep.tile([P, 1], F32, name="total")
         nc.vector.scalar_tensor_tensor(weighted[:], sums[:], 1.0, factor, ALU.subtract, ALU.mult, accum_out=total[:])
         inv = keep.tile([P, 1], F32, name="inv")
         nc.vector.reciprocal(inv[:], total[:])
+
         res = keep.tile([P, S], F32, name="res")
-        for s in (1, 0):
-            nc.vector.tensor_scalar(res[:, spans[s]], ex[:, spans[s]], factor[:, s : s + 1], inv[:], ALU.mult, ALU.mult)
-            nc.sync.dma_start(out[:, spans[s]], res[:, spans[s]])
-        nc.scalar.activation(res[:, spans[2]], ex[:, spans[2]], ACT.Copy, scale=inv[:])
-        nc.scalar.dma_start(out[:, spans[2]], res[:, spans[2]])
+        for s in reversed(range(LAST)):
+            nc.vector.tensor_scalar(res[:, SPANS[s]], ex[:, SPANS[s]], factor[:, s : s + 1], inv[:], ALU.mult, ALU.mult)
+            nc.sync.dma_start(out[:, SPANS[s]], res[:, SPANS[s]])
+        nc.scalar.activation(res[:, SPANS[LAST]], ex[:, SPANS[LAST]], ACT.Copy, scale=inv[:])
+        nc.scalar.dma_start(out[:, SPANS[LAST]], res[:, SPANS[LAST]])

from contextlib import ExitStack

import concourse.mybir as mybir

K, T, S, N = 512, 2048, 1024, 128
FLOPS = 2 * K * S * N

F32 = mybir.dt.float32
BF16 = mybir.dt.bfloat16
I32 = mybir.dt.int32
U32 = mybir.dt.uint32
U16 = mybir.dt.uint16
U8 = mybir.dt.uint8
FP8X4 = mybir.dt.float8_e4m3fn_x4
FP4X4 = mybir.dt.float4_e2m1fn_x4
ALU = mybir.AluOpType
ACT = mybir.ActivationFunctionType
AX = mybir.AxisListType

P = 128
PACK = 4
CHUNK = 256
CHUNKS = S // CHUNK

PLANE2_CUTS = (0, 1024, 2048)
PAIR_CUTS = (0, 1024, 1536, 2048)
PLANE3_CUTS = (0, 512, 1024, 1536, 2048)
PLANE2_VECTOR_CHUNKS = 2
PAIR_SCALAR_COLS = (0, 256, 160)
SPANS = (slice(0, 2 * CHUNK), slice(2 * CHUNK, 3 * CHUNK), slice(3 * CHUNK, 4 * CHUNK))
LAST = len(SPANS) - 1


def pieces(cuts):
    return zip(cuts[:-1], cuts[1:])


def tile_picked_rank_prior_e_kernel(tc, xT, w1_words, w1_scales, prior, offs, out):
    nc = tc.nc
    planes = xT.rearrange("(p t) c -> p t c", t=PACK)
    with ExitStack() as ctx:
        keep = ctx.enter_context(tc.tile_pool(name="keep", bufs=1))
        ring = ctx.enter_context(tc.tile_pool(name="ring", bufs=2))
        psum = ctx.enter_context(tc.psum_pool(name="psum", bufs=1))

        offsets = keep.tile([P, S // 16], U16, name="offsets")

        def chunk_offsets(c):
            return offsets[:, c * CHUNK // 16 : (c + 1) * CHUNK // 16]

        def chunk_cols(c):
            return slice(c * CHUNK, (c + 1) * CHUNK)

        w_scale = keep.tile([P, N], U8, name="w_scale", align_bytes=64)
        nc.vector.memset(w_scale[:].bitcast(I32), 0)

        grouped = [keep.tile([P, CHUNK, PACK], BF16, name="grouped%d" % c, align_bytes=64) for c in range(CHUNKS)]

        raw2 = keep.tile([P, T], F32, name="raw2", tag="raw2_then_plane3")
        plane2 = keep.tile([P, T], BF16, name="plane2")
        for a, b in pieces(PLANE2_CUTS):
            nc.sync.dma_start(raw2[:, a:b], planes[:, 2, a:b])
            nc.scalar.activation(plane2[:, a:b], raw2[:, a:b], ACT.Copy)
        nc.sync.dma_start(offsets[:], offs)
        for c in range(CHUNKS):
            if c < PLANE2_VECTOR_CHUNKS:
                nc.vector.tensor_copy(grouped[c][:, :, 2], raw2[:].indirect(chunk_offsets(c)))
            else:
                nc.scalar.activation(grouped[c][:, :, 2], plane2[:].indirect(chunk_offsets(c)), ACT.Copy)

        pairs = keep.tile([P, T, 2], BF16, name="pairs")
        for (a, b), share in zip(pieces(PAIR_CUTS), PAIR_SCALAR_COLS):
            raw01 = keep.tile([P, 2, b - a], F32, name="raw01_%d" % a)
            nc.sync.dma_start(raw01[:], planes[:, 0:2, a:b])
            mid = b - share
            nc.vector.tensor_copy(
                pairs[:, a:mid, :].rearrange("p (c i) e -> p c e i", i=4),
                raw01[:, :, : mid - a].rearrange("p e (c i) -> p c e i", i=4),
            )
            if mid < b:
                nc.scalar.activation(
                    pairs[:, mid:b, :].rearrange("p (c i) e -> p c e i", i=4),
                    raw01[:, :, mid - a :].rearrange("p e (c i) -> p c e i", i=4),
                    ACT.Copy,
                )
        pair_words = pairs[:].rearrange("p c e -> p (c e)").bitcast(U32)
        for c in range(CHUNKS):
            words = grouped[c][:].rearrange("p j t -> p (j t)").bitcast(U32).rearrange("p (j u) -> p j u", u=2)
            nc.vector.tensor_copy(words[:, :, 0], pair_words.indirect(chunk_offsets(c)))

        plane3 = keep.tile([P, T], BF16, name="plane3", tag="raw2_then_plane3")
        for a, b in pieces(PLANE3_CUTS):
            raw3 = keep.tile([P, b - a], F32, name="raw3_%d" % a)
            nc.sync.dma_start(raw3[:], planes[:, 3, a:b])
            nc.scalar.activation(plane3[:, a:b], raw3[:], ACT.Copy)

        prior_sb = keep.tile([P, S], F32, name="prior_sb")
        nc.sync.dma_start(prior_sb[:], prior)
        w_codes = keep.tile([P, 2 * N], U8, name="w_codes", align_bytes=64)
        nc.sync.dma_start(w_codes[:].bitcast(I32), w1_words[0].bitcast(I32))
        for q in range(4):
            nc.sync.dma_start(w_scale[32 * q : 32 * q + 4, :].bitcast(I32), w1_scales[0, 4 * q : 4 * q + 4, :].bitcast(I32))

        first_max = keep.tile([P, 1], F32, name="first_max")
        sums = keep.tile([P, len(SPANS)], F32, name="sums")
        neg = keep.tile([P, S + len(SPANS)], F32, name="neg")
        ex = keep.tile([P, S + len(SPANS)], F32, name="ex")
        acc = [psum.tile([P, CHUNK], F32, name="acc%d" % c) for c in range(CHUNKS)]
        passed = keep.tile([P, CHUNK], BF16, name="passed")
        neg_max = [first_max[:]] + [neg[:, S + s : S + s + 1] for s in range(len(SPANS))]
        factor = ex[:, S:]
        for c in range(CHUNKS):
            nc.scalar.activation(grouped[c][:, :, 3], plane3[:].indirect(chunk_offsets(c)), ACT.Copy)

        def product(c):
            codes = ring.tile([P, CHUNK], U32, name="codes", align_bytes=64)
            scales = ring.tile([P, CHUNK], U8, name="scales", align_bytes=64)
            nc.vector.quantize_mx(
                out=codes[:].bitcast(FP8X4), scales=scales[:], in_=grouped[c][:].rearrange("p j t -> p (j t)")
            )
            nc.tensor.matmul_mx(
                out=acc[c][:],
                lhsT=w_codes[:].bitcast(FP4X4),
                lhsT_scale=w_scale[:],
                rhs=codes[:].bitcast(FP8X4),
                rhs_scale=scales[:],
                start=True,
                stop=True,
            )

        def add_prior(c):
            cols = chunk_cols(c)
            nc.vector.scalar_tensor_tensor(neg[:, cols], acc[c][:], -1.0, prior_sb[:, cols], ALU.mult, ALU.subtract)

        def running_max(c):
            cols = chunk_cols(c)
            if c == 0:
                nc.vector.tensor_reduce(neg_max[0], neg[:, cols], AX.X, ALU.min)
            else:
                nc.vector.tensor_scalar(passed[:], neg[:, cols], 1.0, neg_max[c - 1], ALU.mult, ALU.min, accum_out=neg_max[c])

        def exponentials(s):
            cols = slice(SPANS[s].start, S + len(SPANS)) if s == LAST else SPANS[s]
            nc.scalar.activation(
                ex[:, cols], neg[:, cols], ACT.Exp, bias=neg_max[s + 1], scale=-1.0, accum_out=sums[:, s : s + 1]
            )

        product(0)
        product(1)
        add_prior(0)
        product(2)
        running_max(0)
        add_prior(1)
        product(3)
        running_max(1)
        exponentials(0)
        add_prior(2)
        add_prior(3)
        running_max(2)
        exponentials(1)
        running_max(3)
        exponentials(2)

        weighted = keep.tile([P, len(SPANS)], F32, name="weighted")
        total = keep.tile([P, 1], F32, name="total")
        nc.vector.scalar_tensor_tensor(weighted[:], sums[:], 1.0, factor, ALU.subtract, ALU.mult, accum_out=total[:])
        inv = keep.tile([P, 1], F32, name="inv")
        nc.vector.reciprocal(inv[:], total[:])

        res = keep.tile([P, S], F32, name="res")
        for s in reversed(range(LAST)):
            nc.vector.tensor_scalar(res[:, SPANS[s]], ex[:, SPANS[s]], factor[:, s : s + 1], inv[:], ALU.mult, ALU.mult)
            nc.sync.dma_start(out[:, SPANS[s]], res[:, SPANS[s]])
        nc.scalar.activation(res[:, SPANS[LAST]], ex[:, SPANS[LAST]], ACT.Copy, scale=inv[:])
        nc.scalar.dma_start(out[:, SPANS[LAST]], res[:, SPANS[LAST]])
